import numpy as np
import ml_dtypes


def mxq(x, axis, fmt="e4m3"):
    dtype, down = {"e4m3": (ml_dtypes.float8_e4m3fn, 7), "e5m2": (ml_dtypes.float8_e5m2, 14)}[fmt]
    v = np.moveaxis(np.asarray(x, np.float32).astype(ml_dtypes.bfloat16).astype(np.float64), axis, -1)
    blocks = v.reshape(v.shape[:-1] + (-1, 32))
    amax = np.abs(blocks).max(-1, keepdims=True)
    byte = np.maximum(np.where(amax > 0, np.frexp(amax)[1] - 1 + 127, 0) - down, 1)
    scale = np.exp2(byte - 127.0)
    codes = (blocks / scale).astype(np.float32).astype(dtype).astype(np.float64)
    return np.moveaxis((codes * scale).reshape(v.shape), -1, axis)


WIDE = False


def mx_kscale(k):
    if not WIDE:
        return np.ones(k)
    levels = np.array([10, -10, 5, -5, 0])
    if k % 512:
        return np.exp2(np.random.permutation(np.resize(levels, k // 32))).repeat(32)
    a = np.empty((k // 512, 16))
    for p in range(k // 512):
        a[p, :8] = np.random.permutation(np.resize(levels, 8))
        for g in range(8):
            far = levels[np.abs(levels - a[p, g]) >= 10]
            a[p, g + 8] = far[np.random.randint(len(far))]
    return np.exp2(a.ravel()).repeat(32)


def f64(x):
    return np.asarray(x).astype(np.float64)


def striped(idx):
    return np.tile(idx.reshape(-1, 16).T, (8, 1)).astype(np.uint16)


def unstriped(offs):
    return offs[:16].T.reshape(-1).astype(np.int64)


def pack_weight(w):
    k, n = w.shape
    w = f64(np.asarray(w, np.float32).astype(ml_dtypes.bfloat16)).reshape(k // 32, 32, n)
    amax = np.abs(w).max(1)
    byte = np.clip(np.where(amax > 0, np.frexp(amax)[1] - 1 + 127 - 7, 1), 1, 254)
    scaled = (w * np.exp2(127.0 - byte)[:, None, :]).reshape(k, n).astype(np.float32)
    words = np.ascontiguousarray(scaled.reshape(k // 512, 128, 4, n).transpose(0, 1, 3, 2)).astype(ml_dtypes.float8_e4m3fn).view(np.uint8)
    return words, np.ascontiguousarray(byte.astype(np.uint8).reshape(k // 512, 16, n))


def unpack_weight(words, scales):
    g, p, n, _ = words.shape
    vals = np.ascontiguousarray(words).view(ml_dtypes.float8_e4m3fn).astype(np.float64) * np.repeat(np.exp2(scales.astype(np.float64) - 127.0), 8, axis=1)[..., None]
    return vals.transpose(0, 1, 3, 2).reshape(g * 512, n)


def sigmoid(v):
    return 1.0 / (1.0 + np.exp(-np.maximum(v, -700.0)))


K, T, S, N, H, U = 512, 2048, 512, 256, 512, 1024


def setup_inputs():
    n = np.random.standard_normal
    s = mx_kscale(K)[:, None]
    u = mx_kscale(H)
    packed_xT = pack_weight(n((K, T)) * s)
    return {
        "x_words": packed_xT[0],
        "x_scales": packed_xT[1],
        "w1": (n((K, H)) / np.sqrt(K) / s).astype(np.float32),
        "w2": (n((K, H)) / np.sqrt(K) / s).astype(np.float32),
        "unit": (np.random.uniform(0.6, 1.4, (H, 1)) * u[:, None]).astype(np.float32),
        "w3": (n((H, N)) / np.sqrt(H) / u[:, None]).astype(np.float32),
        "offs": striped(np.random.permutation(T)[:S]),
        "s1": striped(np.random.permutation(np.concatenate([np.arange(S), np.random.randint(0, S, U - S)]))),
        "s2": striped(np.random.permutation(np.concatenate([np.arange(S), np.random.randint(0, S, U - S)]))),
    }


def reference(x_words, x_scales, w1, w2, unit, w3, offs, s1, s2):
    xq = unpack_weight(x_words, x_scales)[:, unstriped(offs)]
    z1 = mxq(f64(w2), 0, "e4m3").T @ xq
    z_1 = z1[:, unstriped(s1)]
    z_2 = z1[:, unstriped(s2)]
    gate_ = sigmoid(z_1 - z_2)
    y = mxq(f64(w1), 0, "e4m3").T @ xq
    y_1 = y[:, unstriped(s1)]
    y_2 = y[:, unstriped(s2)]
    hid = f64(unit) * (gate_ * y_1 + (-1.0 * gate_ + 1.0) * y_2)
    return mxq(f64(w3), 0, "e4m3").T @ mxq(hid, 0, "e4m3")

@@ -1,0 +1,170 @@
+from contextlib import ExitStack
+
+import concourse.mybir as mybir
+
+K, T, S, N, H, U = 512, 2048, 512, 256, 512, 1024
+FLOPS = 2 * K * H * S * 2 + 2 * H * N * U
+
+F32 = mybir.dt.float32
+BF16 = mybir.dt.bfloat16
+I32 = mybir.dt.int32
+U32 = mybir.dt.uint32
+U16 = mybir.dt.uint16
+U8 = mybir.dt.uint8
+FP8X4 = mybir.dt.float8_e4m3fn_x4
+ALU = mybir.AluOpType
+ACT = mybir.ActivationFunctionType
+
+P = 128
+PACK = 4
+WINDOW = S + 16
+CHUNKS = (256, 512, 256)
+
+
+def tile_picked_yfusgat_gate_p_kernel(tc, x_words, x_scales, w1, w2, unit, w3, offs, s1, s2, out):
+    nc = tc.nc
+    with ExitStack() as ctx:
+        keep = ctx.enter_context(tc.tile_pool(name="keep", bufs=1))
+        psum = ctx.enter_context(tc.psum_pool(name="psum", bufs=4))
+
+        offs_sb = keep.tile([P, S // 16], U16, name="offs_sb")
+        s1_sb = keep.tile([P, U // 16], U16, name="s1_sb")
+        s2_sb = keep.tile([P, U // 16], U16, name="s2_sb")
+        x_word_table = keep.tile([P, T], I32, name="x_word_table")
+        x_scale_table = keep.tile([P, T], U8, name="x_scale_table")
+        w1_raw = keep.tile([P, PACK, H], F32, name="w1_raw")
+        w2_raw = keep.tile([P, PACK, H], F32, name="w2_raw")
+        w3_raw = keep.tile([P, PACK, N], F32, name="w3_raw")
+        unit_sb = keep.tile([P, PACK], F32, name="unit_sb")
+
+        nc.gpsimd.memset(x_scale_table[:].bitcast(I32), 0)
+        nc.sync.dma_start(offs_sb[:], offs)
+        nc.sync.dma_start(w2_raw[:], w2.rearrange("(p j) c -> p j c", j=PACK))
+        for q in range(4):
+            nc.sync.dma_start(
+                x_scale_table[32 * q : 32 * q + 4, :].bitcast(I32),
+                x_scales[0, 4 * q : 4 * q + 4, :].bitcast(I32),
+            )
+        nc.sync.dma_start(x_word_table[:], x_words[0].rearrange("p c r -> p (c r)").bitcast(I32))
+        nc.sync.dma_start(s2_sb[:], s2)
+        nc.sync.dma_start(w1_raw[:], w1.rearrange("(p j) c -> p j c", j=PACK))
+        nc.sync.dma_start(s1_sb[:], s1)
+        nc.sync.dma_start(unit_sb[:], unit.rearrange("(p t) o -> p (t o)", t=PACK))
+        nc.sync.dma_start(w3_raw[:], w3.rearrange("(p j) n -> p j n", j=PACK))
+
+        z_rows = [keep.tile([P, WINDOW], F32, name=f"z_rows{t}") for t in range(PACK)]
+        y_rows = [keep.tile([P, WINDOW], F32, name=f"y_rows{t}") for t in range(PACK)]
+        for rows in z_rows + y_rows:
+            nc.gpsimd.memset(rows[:, S:], 0.0)
+
+        x_scale_picked = keep.tile([P, S], U8, name="x_scale_picked", align_bytes=64)
+        x_word_picked = keep.tile([P, S], U32, name="x_word_picked", align_bytes=64)
+        nc.vector.tensor_copy(x_scale_picked[:], x_scale_table[:].indirect(offs_sb[:]))
+
+        def quantise(name, grouped, width):
+            codes = keep.tile([P, width], U32, name=name + "_codes", align_bytes=64)
+            scales = keep.tile([P, width], U8, name=name + "_scales", align_bytes=64)
+            nc.vector.quantize_mx(out=codes[:].bitcast(FP8X4), scales=scales[:], in_=grouped[:])
+            return codes, scales
+
+        def dealt_views(grouped, raw):
+            return (
+                grouped[:].rearrange("p (t m j) -> p m j t", t=PACK, j=PACK),
+                raw[:].rearrange("p j (m t) -> p m j t", t=PACK),
+            )
+
+        w2_grouped = keep.tile([P, PACK * H], BF16, name="w2_grouped", align_bytes=64)
+        dst, src = dealt_views(w2_grouped, w2_raw)
+        nc.vector.tensor_copy(dst[:, :84], src[:, :84])
+        nc.scalar.copy(dst[:, 84:], src[:, 84:])
+        w2_codes, w2_scales = quantise("w2", w2_grouped, H)
+        nc.vector.tensor_copy(x_word_picked[:], x_word_table[:].bitcast(U32).indirect(offs_sb[:]))
+
+        def project(codes, scales, t):
+            bank = psum.tile([P, S], F32, name="proj_bank")
+            cols = slice(t * P, (t + 1) * P)
+            nc.tensor.matmul_mx(
+                out=bank[:],
+                lhsT=codes[:, cols].bitcast(FP8X4),
+                lhsT_scale=scales[:, cols],
+                rhs=x_word_picked[:].bitcast(FP8X4),
+                rhs_scale=x_scale_picked[:],
+                start=True,
+                stop=True,
+            )
+            return bank
+
+        z_banks = [project(w2_codes, w2_scales, t) for t in range(PACK)]
+
+        w1_grouped = keep.tile([P, PACK * H], BF16, name="w1_grouped", align_bytes=64)
+        dst, src = dealt_views(w1_grouped, w1_raw)
+        nc.vector.tensor_copy(dst, src)
+        w1_codes, w1_scales = quantise("w1", w1_grouped, H)
+
+        r0 = 0
+        for c, n in enumerate(CHUNKS):
+            first = s1_sb[:, r0 // 16 : (r0 + n) // 16]
+            second = s2_sb[:, r0 // 16 : (r0 + n) // 16]
+            gates = []
+            for t in range(PACK):
+                if c == 0:
+                    nc.scalar.copy(z_rows[t][:, :S], z_banks[t][:])
+                z2_neg = keep.tile([P, n], F32, name=f"z2_neg{c}_{t}")
+                nc.scalar.activation(z2_neg[:], z_rows[t][:].indirect(second), ACT.Copy, scale=-1.0)
+                diff = keep.tile([P, n], F32, name=f"diff{c}_{t}")
+                nc.vector.tensor_tensor(diff[:], z_rows[t][:].indirect(first), z2_neg[:], ALU.add)
+                gates.append(diff)
+            y2_neg = keep.tile([P, PACK, n], F32, name=f"y2_neg{c}")
+            mixed = keep.tile([P, PACK, n], F32, name=f"mixed{c}")
+            for t in range(PACK):
+                if c == 0:
+                    bank = project(w1_codes, w1_scales, t)
+                    if t % 2 == 0:
+                        nc.scalar.activation(y_rows[t][:, :S], bank[:], ACT.Copy, scale=unit_sb[:, t : t + 1])
+                    else:
+                        nc.vector.tensor_scalar(y_rows[t][:, :S], bank[:], unit_sb[:, t : t + 1], None, ALU.mult)
+                nc.scalar.activation(y2_neg[:, t, :], y_rows[t][:].indirect(second), ACT.Copy, scale=-1.0)
+                gate = keep.tile([P, n], F32, name=f"gate{c}_{t}")
+                nc.scalar.activation(gate[:], gates[t][:], ACT.Sigmoid)
+                y_diff = keep.tile([P, n], F32, name=f"y_diff{c}_{t}")
+                if c == len(CHUNKS) - 1:
+                    y1 = keep.tile([P, n], F32, name=f"y1_{t}")
+                    nc.scalar.activation(y1[:], y_rows[t][:].indirect(first), ACT.Copy)
+                    nc.vector.tensor_tensor(y_diff[:], y1[:], y2_neg[:, t, :], ALU.add)
+                else:
+                    nc.vector.tensor_tensor(y_diff[:], y_rows[t][:].indirect(first), y2_neg[:, t, :], ALU.add)
+                nc.vector.tensor_tensor(mixed[:, t, :], gate[:], y_diff[:], ALU.mult)
+            if c == 0:
+                w3_grouped = keep.tile([P, PACK * N], BF16, name="w3_grouped", align_bytes=64)
+                nc.vector.tensor_copy(
+                    w3_grouped[:].rearrange("p (c i j) -> p c j i", i=4, j=PACK),
+                    w3_raw[:].rearrange("p j (c i) -> p c j i", i=4),
+                )
+                w3_codes, w3_scales = quantise("w3", w3_grouped, N)
+            hid = keep.tile([P, PACK * n], BF16, name=f"hid{c}", align_bytes=64)
+            nc.vector.tensor_tensor(
+                hid[:].rearrange("p (c i t) -> p c t i", i=4, t=PACK),
+                mixed[:].rearrange("p t (c i) -> p c t i", i=4),
+                y2_neg[:].rearrange("p t (c i) -> p c t i", i=4),
+                ALU.subtract,
+            )
+            hid_codes, hid_scales = quantise(f"hid{c}", hid, n)
+            for m in range(N // P):
+                rows = slice(m * P, (m + 1) * P)
+                bank = psum.tile([P, n], F32, name="out_bank")
+                nc.tensor.matmul_mx(
+                    out=bank[:],
+                    lhsT=w3_codes[:, rows].bitcast(FP8X4),
+                    lhsT_scale=w3_scales[:, rows],
+                    rhs=hid_codes[:].bitcast(FP8X4),
+                    rhs_scale=hid_scales[:],
+                    start=True,
+                    stop=True,
+                )
+                result = keep.tile([P, n], F32, name=f"result{c}_{m}")
+                if c == len(CHUNKS) - 1 and m == 1:
+                    nc.vector.tensor_copy(result[:], bank[:])
+                else:
+                    nc.scalar.copy(result[:], bank[:])
+                nc.sync.dma_start(out[rows, r0 : r0 + n], result[:])
+            r0 = r0 + n

@@ -19,35 +19,44 @@ P = 128
 PACK = 4
 WINDOW = S + 16
 CHUNKS = (256, 512, 256)
+Z_OUT = "SVSS"
+Y_OUT = "VSVS"
+Y_EARLY = 0
+UNFUSED = (2, 3)
+LINE = 4
 
 
 def tile_picked_yfusgat_gate_p_kernel(tc, x_words, x_scales, w1, w2, unit, w3, offs, s1, s2, out):
     nc = tc.nc
     with ExitStack() as ctx:
         keep = ctx.enter_context(tc.tile_pool(name="keep", bufs=1))
-        psum = ctx.enter_context(tc.psum_pool(name="psum", bufs=4))
+        psum = ctx.enter_context(tc.psum_pool(name="psum", bufs=8))
 
         offs_sb = keep.tile([P, S // 16], U16, name="offs_sb")
         s1_sb = keep.tile([P, U // 16], U16, name="s1_sb")
         s2_sb = keep.tile([P, U // 16], U16, name="s2_sb")
         x_word_table = keep.tile([P, T], I32, name="x_word_table")
         x_scale_table = keep.tile([P, T], U8, name="x_scale_table")
-        w1_raw = keep.tile([P, PACK, H], F32, name="w1_raw")
-        w2_raw = keep.tile([P, PACK, H], F32, name="w2_raw")
+        w1_raw = [keep.tile([P, PACK, H // 2], F32, name=f"w1_raw{h}") for h in range(2)]
+        w2_raw = [keep.tile([P, PACK, H // 2], F32, name=f"w2_raw{h}") for h in range(2)]
         w3_raw = keep.tile([P, PACK, N], F32, name="w3_raw")
         unit_sb = keep.tile([P, PACK], F32, name="unit_sb")
 
         nc.gpsimd.memset(x_scale_table[:].bitcast(I32), 0)
+        w2_rows = w2.rearrange("(p j) c -> p j c", j=PACK)
+        nc.sync.dma_start(w2_raw[0][:], w2_rows[:, :, : H // 2])
+        nc.sync.dma_start(w2_raw[1][:], w2_rows[:, :, H // 2 :])
         nc.sync.dma_start(offs_sb[:], offs)
-        nc.sync.dma_start(w2_raw[:], w2.rearrange("(p j) c -> p j c", j=PACK))
         for q in range(4):
             nc.sync.dma_start(
                 x_scale_table[32 * q : 32 * q + 4, :].bitcast(I32),
                 x_scales[0, 4 * q : 4 * q + 4, :].bitcast(I32),
             )
         nc.sync.dma_start(x_word_table[:], x_words[0].rearrange("p c r -> p (c r)").bitcast(I32))
+        w1_rows = w1.rearrange("(p j) c -> p j c", j=PACK)
+        nc.sync.dma_start(w1_raw[0][:], w1_rows[:, :, : H // 2])
         nc.sync.dma_start(s2_sb[:], s2)
-        nc.sync.dma_start(w1_raw[:], w1.rearrange("(p j) c -> p j c", j=PACK))
+        nc.sync.dma_start(w1_raw[1][:], w1_rows[:, :, H // 2 :])
         nc.sync.dma_start(s1_sb[:], s1)
         nc.sync.dma_start(unit_sb[:], unit.rearrange("(p t) o -> p (t o)", t=PACK))
         nc.sync.dma_start(w3_raw[:], w3.rearrange("(p j) n -> p j n", j=PACK))
@@ -64,107 +73,122 @@ def tile_picked_yfusgat_gate_p_kernel(tc, x_words, x_scales, w1, w2, unit, w3, o
         def quantise(name, grouped, width):
             codes = keep.tile([P, width], U32, name=name + "_codes", align_bytes=64)
             scales = keep.tile([P, width], U8, name=name + "_scales", align_bytes=64)
-            nc.vector.quantize_mx(out=codes[:].bitcast(FP8X4), scales=scales[:], in_=grouped[:])
+            nc.vector.quantize_mx(out=codes[:].bitcast(FP8X4), scales=scales[:], in_=grouped)
             return codes, scales
 
-        def dealt_views(grouped, raw):
-            return (
-                grouped[:].rearrange("p (t m j) -> p m j t", t=PACK, j=PACK),
-                raw[:].rearrange("p j (m t) -> p m j t", t=PACK),
-            )
-
-        w2_grouped = keep.tile([P, PACK * H], BF16, name="w2_grouped", align_bytes=64)
-        dst, src = dealt_views(w2_grouped, w2_raw)
-        nc.vector.tensor_copy(dst[:, :84], src[:, :84])
-        nc.scalar.copy(dst[:, 84:], src[:, 84:])
-        w2_codes, w2_scales = quantise("w2", w2_grouped, H)
-        nc.vector.tensor_copy(x_word_picked[:], x_word_table[:].bitcast(U32).indirect(offs_sb[:]))
-
-        def project(codes, scales, t):
-            bank = psum.tile([P, S], F32, name="proj_bank")
-            cols = slice(t * P, (t + 1) * P)
+        def product(lhs, lhs_cols, rhs, rhs_cols, width):
+            bank = psum.tile([P, width], F32, name="bank")
             nc.tensor.matmul_mx(
                 out=bank[:],
-                lhsT=codes[:, cols].bitcast(FP8X4),
-                lhsT_scale=scales[:, cols],
-                rhs=x_word_picked[:].bitcast(FP8X4),
-                rhs_scale=x_scale_picked[:],
+                lhsT=lhs[0][:, lhs_cols].bitcast(FP8X4),
+                lhsT_scale=lhs[1][:, lhs_cols],
+                rhs=rhs[0][:, rhs_cols].bitcast(FP8X4),
+                rhs_scale=rhs[1][:, rhs_cols],
                 start=True,
                 stop=True,
             )
             return bank
 
-        z_banks = [project(w2_codes, w2_scales, t) for t in range(PACK)]
+        def dealt(grouped):
+            return grouped[:].rearrange("p (t m j) -> p m j t", t=PACK, j=PACK)
 
-        w1_grouped = keep.tile([P, PACK * H], BF16, name="w1_grouped", align_bytes=64)
-        dst, src = dealt_views(w1_grouped, w1_raw)
-        nc.vector.tensor_copy(dst, src)
-        w1_codes, w1_scales = quantise("w1", w1_grouped, H)
+        def by_line(raw):
+            return raw[:].rearrange("p j (m t) -> p m j t", t=PACK)
+
+        w2_grouped = keep.tile([P, PACK * H], BF16, name="w2_grouped", align_bytes=64)
+        nc.scalar.copy(dealt(w2_grouped)[:, :64], by_line(w2_raw[0]))
+        nc.vector.tensor_copy(dealt(w2_grouped)[:, 64:], by_line(w2_raw[1]))
+        w2_mx = quantise("w2", w2_grouped[:], H)
+        halves = [slice(h * S // 2, (h + 1) * S // 2) for h in range(2)]
+        for h, cols in enumerate(halves):
+            nc.vector.tensor_copy(
+                x_word_picked[:, cols], x_word_table[:].bitcast(U32).indirect(offs_sb[:, h * 16 : (h + 1) * 16])
+            )
+        x_mx = (x_word_picked, x_scale_picked)
+
+        planes = [slice(t * P, (t + 1) * P) for t in range(PACK)]
+        z_banks = [[(cols, product(w2_mx, planes[0], x_mx, cols, S // 2)) for cols in halves]]
+        for t in range(1, PACK):
+            z_banks.append([(slice(0, S), product(w2_mx, planes[t], x_mx, slice(0, S), S))])
+
+        w1_grouped = keep.tile([P, PACK * H], BF16, name="w1_grouped", tag="w1_grouped", align_bytes=64)
+        for h in range(2):
+            nc.vector.tensor_copy(dealt(w1_grouped)[:, h * 64 : (h + 1) * 64], by_line(w1_raw[h]))
+        w1_mx = quantise("w1", w1_grouped[:], H)
+        y_banks = [product(w1_mx, planes[t], x_mx, slice(0, S), S) for t in range(PACK)]
+
+        w3_grouped = keep.tile([P, PACK * N], BF16, name="w3_grouped", align_bytes=64)
+        nc.vector.tensor_copy(
+            w3_grouped[:].rearrange("p (c i j) -> p c j i", i=4, j=PACK),
+            w3_raw[:].rearrange("p j (c i) -> p c j i", i=4),
+        )
+        w3_mx = quantise("w3", w3_grouped[:], N)
+        first_diffs = keep.tile([P, PACK, CHUNKS[0]], F32, name="first_diffs", tag="w1_grouped", align_bytes=64)
+
+        def y_out(t):
+            if Y_OUT[t] == "S":
+                nc.scalar.activation(y_rows[t][:, :S], y_banks[t][:], ACT.Copy, scale=unit_sb[:, t : t + 1])
+            else:
+                nc.vector.tensor_scalar(y_rows[t][:, :S], y_banks[t][:], unit_sb[:, t : t + 1], None, ALU.mult)
 
         r0 = 0
         for c, n in enumerate(CHUNKS):
+            last = c == len(CHUNKS) - 1
             first = s1_sb[:, r0 // 16 : (r0 + n) // 16]
             second = s2_sb[:, r0 // 16 : (r0 + n) // 16]
-            gates = []
+            diffs = []
             for t in range(PACK):
                 if c == 0:
-                    nc.scalar.copy(z_rows[t][:, :S], z_banks[t][:])
-                z2_neg = keep.tile([P, n], F32, name=f"z2_neg{c}_{t}")
+                    for cols, bank in z_banks[t]:
+                        if Z_OUT[t] == "S":
+                            nc.scalar.copy(z_rows[t][:, cols], bank[:])
+                        else:
+                            nc.vector.tensor_copy(z_rows[t][:, cols], bank[:])
+                z2_neg = keep.tile([P, n], F32, name=f"z2_neg{c}_{t}", tag=f"pair{t}")
                 nc.scalar.activation(z2_neg[:], z_rows[t][:].indirect(second), ACT.Copy, scale=-1.0)
-                diff = keep.tile([P, n], F32, name=f"diff{c}_{t}")
-                nc.vector.tensor_tensor(diff[:], z_rows[t][:].indirect(first), z2_neg[:], ALU.add)
-                gates.append(diff)
+                if c == 0:
+                    diff = first_diffs[:, t, :]
+                else:
+                    diff = keep.tile([P, n], F32, name=f"diff{c}_{t}", tag=f"diff{c}_{t}")[:]
+                nc.vector.tensor_tensor(diff, z_rows[t][:].indirect(first), z2_neg[:], ALU.add)
+                diffs.append(diff)
+                if c == 0 and t >= PACK - Y_EARLY:
+                    y_out(t - (PACK - Y_EARLY))
             y2_neg = keep.tile([P, PACK, n], F32, name=f"y2_neg{c}")
             mixed = keep.tile([P, PACK, n], F32, name=f"mixed{c}")
             for t in range(PACK):
-                if c == 0:
-                    bank = project(w1_codes, w1_scales, t)
-                    if t % 2 == 0:
-                        nc.scalar.activation(y_rows[t][:, :S], bank[:], ACT.Copy, scale=unit_sb[:, t : t + 1])
-                    else:
-                        nc.vector.tensor_scalar(y_rows[t][:, :S], bank[:], unit_sb[:, t : t + 1], None, ALU.mult)
+                if c == 0 and t >= Y_EARLY:
+                    y_out(t)
                 nc.scalar.activation(y2_neg[:, t, :], y_rows[t][:].indirect(second), ACT.Copy, scale=-1.0)
                 gate = keep.tile([P, n], F32, name=f"gate{c}_{t}")
-                nc.scalar.activation(gate[:], gates[t][:], ACT.Sigmoid)
-                y_diff = keep.tile([P, n], F32, name=f"y_diff{c}_{t}")
-                if c == len(CHUNKS) - 1:
-                    y1 = keep.tile([P, n], F32, name=f"y1_{t}")
+                nc.scalar.activation(gate[:], diffs[t], ACT.Sigmoid)
+                y_diff = keep.tile([P, n], F32, name=f"y_diff{c}_{t}", tag=f"pair{t}")
+                if last and t in UNFUSED:
+                    y1 = keep.tile([P, n], F32, name=f"y1_{t}", tag=f"diff{c - 1}_{t}")
                     nc.scalar.activation(y1[:], y_rows[t][:].indirect(first), ACT.Copy)
                     nc.vector.tensor_tensor(y_diff[:], y1[:], y2_neg[:, t, :], ALU.add)
                 else:
                     nc.vector.tensor_tensor(y_diff[:], y_rows[t][:].indirect(first), y2_neg[:, t, :], ALU.add)
                 nc.vector.tensor_tensor(mixed[:, t, :], gate[:], y_diff[:], ALU.mult)
-            if c == 0:
-                w3_grouped = keep.tile([P, PACK * N], BF16, name="w3_grouped", align_bytes=64)
-                nc.vector.tensor_copy(
-                    w3_grouped[:].rearrange("p (c i j) -> p c j i", i=4, j=PACK),
-                    w3_raw[:].rearrange("p j (c i) -> p c j i", i=4),
+            pieces = [(0, n // 2), (n // 2, n // 2)] if last else [(0, n)]
+            hids = []
+            for a, w in pieces:
+                hid = keep.tile([P, PACK * w], BF16, name=f"hid{c}_{a}", align_bytes=64)
+                nc.vector.tensor_tensor(
+                    hid[:].rearrange("p (c i t) -> p c t i", i=LINE, t=PACK),
+                    mixed[:, :, a : a + w].rearrange("p t (c i) -> p c t i", i=LINE),
+                    y2_neg[:, :, a : a + w].rearrange("p t (c i) -> p c t i", i=LINE),
+                    ALU.subtract,
                 )
-                w3_codes, w3_scales = quantise("w3", w3_grouped, N)
-            hid = keep.tile([P, PACK * n], BF16, name=f"hid{c}", align_bytes=64)
-            nc.vector.tensor_tensor(
-                hid[:].rearrange("p (c i t) -> p c t i", i=4, t=PACK),
-                mixed[:].rearrange("p t (c i) -> p c t i", i=4),
-                y2_neg[:].rearrange("p t (c i) -> p c t i", i=4),
-                ALU.subtract,
-            )
-            hid_codes, hid_scales = quantise(f"hid{c}", hid, n)
-            for m in range(N // P):
-                rows = slice(m * P, (m + 1) * P)
-                bank = psum.tile([P, n], F32, name="out_bank")
-                nc.tensor.matmul_mx(
-                    out=bank[:],
-                    lhsT=w3_codes[:, rows].bitcast(FP8X4),
-                    lhsT_scale=w3_scales[:, rows],
-                    rhs=hid_codes[:].bitcast(FP8X4),
-                    rhs_scale=hid_scales[:],
-                    start=True,
-                    stop=True,
-                )
-                result = keep.tile([P, n], F32, name=f"result{c}_{m}")
-                if c == len(CHUNKS) - 1 and m == 1:
-                    nc.vector.tensor_copy(result[:], bank[:])
-                else:
-                    nc.scalar.copy(result[:], bank[:])
-                nc.sync.dma_start(out[rows, r0 : r0 + n], result[:])
+                hids.append(hid)
+            for (a, w), hid in zip(pieces, hids):
+                hid_mx = quantise(f"hid{c}_{a}", hid[:], w)
+                for m in range(N // P):
+                    bank = product(w3_mx, planes[m], hid_mx, slice(0, w), w)
+                    result = keep.tile([P, w], F32, name=f"result{c}_{a}_{m}")
+                    if last and a > 0 and m == 1:
+                        nc.vector.tensor_copy(result[:], bank[:])
+                    else:
+                        nc.scalar.copy(result[:], bank[:])
+                    nc.sync.dma_start(out[planes[m], r0 + a : r0 + a + w], result[:])
             r0 = r0 + n

@@ -19,10 +19,10 @@ P = 128
 PACK = 4
 WINDOW = S + 16
 CHUNKS = (256, 512, 256)
-Z_OUT = "SVSS"
-Y_OUT = "VSVS"
+Z_OUT = "SVSV"
+Y_OUT = "SSSS"
 Y_EARLY = 0
-UNFUSED = (2, 3)
+UNFUSED = (0, 1, 2, 3)
 LINE = 4
 
 
@@ -45,13 +45,13 @@ def tile_picked_yfusgat_gate_p_kernel(tc, x_words, x_scales, w1, w2, unit, w3, o
         nc.gpsimd.memset(x_scale_table[:].bitcast(I32), 0)
         w2_rows = w2.rearrange("(p j) c -> p j c", j=PACK)
         nc.sync.dma_start(w2_raw[0][:], w2_rows[:, :, : H // 2])
-        nc.sync.dma_start(w2_raw[1][:], w2_rows[:, :, H // 2 :])
         nc.sync.dma_start(offs_sb[:], offs)
         for q in range(4):
             nc.sync.dma_start(
                 x_scale_table[32 * q : 32 * q + 4, :].bitcast(I32),
                 x_scales[0, 4 * q : 4 * q + 4, :].bitcast(I32),
             )
+        nc.sync.dma_start(w2_raw[1][:], w2_rows[:, :, H // 2 :])
         nc.sync.dma_start(x_word_table[:], x_words[0].rearrange("p c r -> p (c r)").bitcast(I32))
         w1_rows = w1.rearrange("(p j) c -> p j c", j=PACK)
         nc.sync.dma_start(w1_raw[0][:], w1_rows[:, :, : H // 2])
@@ -159,6 +159,14 @@ def tile_picked_yfusgat_gate_p_kernel(tc, x_words, x_scales, w1, w2, unit, w3, o
             for t in range(PACK):
                 if c == 0 and t >= Y_EARLY:
                     y_out(t)
+                if c == 0:
+                    gate = keep.tile([P, n], F32, name=f"gate{c}_{t}", tag=f"pair{t}")
+                    nc.scalar.activation(gate[:], diffs[t], ACT.Sigmoid)
+                    other_gate = keep.tile([P, n], F32, name=f"other_gate{t}")
+                    nc.scalar.activation(other_gate[:], diffs[t], ACT.Sigmoid, scale=-1.0)
+                    nc.vector.tensor_tensor(mixed[:, t, :], y_rows[t][:].indirect(first), gate[:], ALU.mult)
+                    nc.vector.tensor_tensor(y2_neg[:, t, :], y_rows[t][:].indirect(second), other_gate[:], ALU.mult)
+                    continue
                 nc.scalar.activation(y2_neg[:, t, :], y_rows[t][:].indirect(second), ACT.Copy, scale=-1.0)
                 gate = keep.tile([P, n], F32, name=f"gate{c}_{t}")
                 nc.scalar.activation(gate[:], diffs[t], ACT.Sigmoid)
@@ -178,7 +186,7 @@ def tile_picked_yfusgat_gate_p_kernel(tc, x_words, x_scales, w1, w2, unit, w3, o
                     hid[:].rearrange("p (c i t) -> p c t i", i=LINE, t=PACK),
                     mixed[:, :, a : a + w].rearrange("p t (c i) -> p c t i", i=LINE),
                     y2_neg[:, :, a : a + w].rearrange("p t (c i) -> p c t i", i=LINE),
-                    ALU.subtract,
+                    ALU.add if c == 0 else ALU.subtract,
                 )
                 hids.append(hid)
             for (a, w), hid in zip(pieces, hids):

@@ -23,7 +23,7 @@ Z_OUT = "SVSV"
 Y_OUT = "SSSS"
 Y_EARLY = 0
 UNFUSED = (0, 1, 2, 3)
-LINE = 4
+LINE = 2
 
 
 def tile_picked_yfusgat_gate_p_kernel(tc, x_words, x_scales, w1, w2, unit, w3, offs, s1, s2, out):
@@ -48,8 +48,8 @@ def tile_picked_yfusgat_gate_p_kernel(tc, x_words, x_scales, w1, w2, unit, w3, o
         nc.sync.dma_start(offs_sb[:], offs)
         for q in range(4):
             nc.sync.dma_start(
-                x_scale_table[32 * q : 32 * q + 4, :].bitcast(I32),
-                x_scales[0, 4 * q : 4 * q + 4, :].bitcast(I32),
+                x_scale_table[q:P:32, :].bitcast(I32),
+                x_scales[0, q:16:4, :].bitcast(I32),
             )
         nc.sync.dma_start(w2_raw[1][:], w2_rows[:, :, H // 2 :])
         nc.sync.dma_start(x_word_table[:], x_words[0].rearrange("p c r -> p (c r)").bitcast(I32))
@@ -119,8 +119,8 @@ def tile_picked_yfusgat_gate_p_kernel(tc, x_words, x_scales, w1, w2, unit, w3, o
 
         w3_grouped = keep.tile([P, PACK * N], BF16, name="w3_grouped", align_bytes=64)
         nc.vector.tensor_copy(
-            w3_grouped[:].rearrange("p (c i j) -> p c j i", i=4, j=PACK),
-            w3_raw[:].rearrange("p j (c i) -> p c j i", i=4),
+            w3_grouped[:].rearrange("p (c i j) -> p c j i", i=LINE, j=PACK),
+            w3_raw[:].rearrange("p j (c i) -> p c j i", i=LINE),
         )
         w3_mx = quantise("w3", w3_grouped[:], N)
         first_diffs = keep.tile([P, PACK, CHUNKS[0]], F32, name="first_diffs", tag="w1_grouped", align_bytes=64)

@@ -17,27 +17,26 @@ ACT = mybir.ActivationFunctionType
 
 P = 128
 PACK = 4
-WINDOW = S + 16
+GROUP = 16
+QUADRANT = 32
+BANKS = 8
+WINDOW = S + GROUP
 CHUNKS = (256, 512, 256)
-Z_OUT = "SVSV"
-Y_OUT = "SSSS"
-Y_EARLY = 0
-UNFUSED = (0, 1, 2, 3)
-LINE = 2
+RUN = 2
 
 
 def tile_picked_yfusgat_gate_p_kernel(tc, x_words, x_scales, w1, w2, unit, w3, offs, s1, s2, out):
     nc = tc.nc
     with ExitStack() as ctx:
         keep = ctx.enter_context(tc.tile_pool(name="keep", bufs=1))
-        psum = ctx.enter_context(tc.psum_pool(name="psum", bufs=8))
+        psum = ctx.enter_context(tc.psum_pool(name="psum", bufs=BANKS))
 
-        offs_sb = keep.tile([P, S // 16], U16, name="offs_sb")
-        s1_sb = keep.tile([P, U // 16], U16, name="s1_sb")
-        s2_sb = keep.tile([P, U // 16], U16, name="s2_sb")
+        offs_sb = keep.tile([P, S // GROUP], U16, name="offs_sb")
+        s1_sb = keep.tile([P, U // GROUP], U16, name="s1_sb")
+        s2_sb = keep.tile([P, U // GROUP], U16, name="s2_sb")
         x_word_table = keep.tile([P, T], I32, name="x_word_table")
         x_scale_table = keep.tile([P, T], U8, name="x_scale_table")
-        w1_raw = [keep.tile([P, PACK, H // 2], F32, name=f"w1_raw{h}") for h in range(2)]
+        w1_raw = [keep.tile([P, PACK, H // 2], F32, name=f"w1_raw{h}", tag=f"w1_raw{h}") for h in range(2)]
         w2_raw = [keep.tile([P, PACK, H // 2], F32, name=f"w2_raw{h}") for h in range(2)]
         w3_raw = keep.tile([P, PACK, N], F32, name="w3_raw")
         unit_sb = keep.tile([P, PACK], F32, name="unit_sb")
@@ -46,10 +45,10 @@ def tile_picked_yfusgat_gate_p_kernel(tc, x_words, x_scales, w1, w2, unit, w3, o
         w2_rows = w2.rearrange("(p j) c -> p j c", j=PACK)
         nc.sync.dma_start(w2_raw[0][:], w2_rows[:, :, : H // 2])
         nc.sync.dma_start(offs_sb[:], offs)
-        for q in range(4):
+        for r in range(PACK):
             nc.sync.dma_start(
-                x_scale_table[q:P:32, :].bitcast(I32),
-                x_scales[0, q:16:4, :].bitcast(I32),
+                x_scale_table[r:P:QUADRANT, :].bitcast(I32),
+                x_scales[0, r : K // 32 : PACK, :].bitcast(I32),
             )
         nc.sync.dma_start(w2_raw[1][:], w2_rows[:, :, H // 2 :])
         nc.sync.dma_start(x_word_table[:], x_words[0].rearrange("p c r -> p (c r)").bitcast(I32))
@@ -61,7 +60,7 @@ def tile_picked_yfusgat_gate_p_kernel(tc, x_words, x_scales, w1, w2, unit, w3, o
         nc.sync.dma_start(unit_sb[:], unit.rearrange("(p t) o -> p (t o)", t=PACK))
         nc.sync.dma_start(w3_raw[:], w3.rearrange("(p j) n -> p j n", j=PACK))
 
-        z_rows = [keep.tile([P, WINDOW], F32, name=f"z_rows{t}") for t in range(PACK)]
+        z_rows = [keep.tile([P, WINDOW], F32, name=f"z_rows{t}") for t in range(PACK - 1)]
         y_rows = [keep.tile([P, WINDOW], F32, name=f"y_rows{t}") for t in range(PACK)]
         for rows in z_rows + y_rows:
             nc.gpsimd.memset(rows[:, S:], 0.0)
@@ -71,10 +70,10 @@ def tile_picked_yfusgat_gate_p_kernel(tc, x_words, x_scales, w1, w2, unit, w3, o
         nc.vector.tensor_copy(x_scale_picked[:], x_scale_table[:].indirect(offs_sb[:]))
 
         def quantise(name, grouped, width):
-            codes = keep.tile([P, width], U32, name=name + "_codes", align_bytes=64)
+            words = keep.tile([P, width], U32, name=name + "_words", align_bytes=64)
             scales = keep.tile([P, width], U8, name=name + "_scales", align_bytes=64)
-            nc.vector.quantize_mx(out=codes[:].bitcast(FP8X4), scales=scales[:], in_=grouped)
-            return codes, scales
+            nc.vector.quantize_mx(out=words[:].bitcast(FP8X4), scales=scales[:], in_=grouped)
+            return words, scales
 
         def product(lhs, lhs_cols, rhs, rhs_cols, width):
             bank = psum.tile([P, width], F32, name="bank")
@@ -92,111 +91,112 @@ def tile_picked_yfusgat_gate_p_kernel(tc, x_words, x_scales, w1, w2, unit, w3, o
         def dealt(grouped):
             return grouped[:].rearrange("p (t m j) -> p m j t", t=PACK, j=PACK)
 
-        def by_line(raw):
+        def by_fours(raw):
             return raw[:].rearrange("p j (m t) -> p m j t", t=PACK)
 
         w2_grouped = keep.tile([P, PACK * H], BF16, name="w2_grouped", align_bytes=64)
-        nc.scalar.copy(dealt(w2_grouped)[:, :64], by_line(w2_raw[0]))
-        nc.vector.tensor_copy(dealt(w2_grouped)[:, 64:], by_line(w2_raw[1]))
+        nc.scalar.copy(dealt(w2_grouped)[:, : P // 2], by_fours(w2_raw[0]))
+        nc.vector.tensor_copy(dealt(w2_grouped)[:, P // 2 :], by_fours(w2_raw[1]))
         w2_mx = quantise("w2", w2_grouped[:], H)
+
         halves = [slice(h * S // 2, (h + 1) * S // 2) for h in range(2)]
-        for h, cols in enumerate(halves):
+        for cols in halves:
             nc.vector.tensor_copy(
-                x_word_picked[:, cols], x_word_table[:].bitcast(U32).indirect(offs_sb[:, h * 16 : (h + 1) * 16])
+                x_word_picked[:, cols],
+                x_word_table[:].bitcast(U32).indirect(offs_sb[:, cols.start // GROUP : cols.stop // GROUP]),
             )
         x_mx = (x_word_picked, x_scale_picked)
 
-        planes = [slice(t * P, (t + 1) * P) for t in range(PACK)]
-        z_banks = [[(cols, product(w2_mx, planes[0], x_mx, cols, S // 2)) for cols in halves]]
+        picked = slice(0, S)
+        blocks = [slice(b * P, (b + 1) * P) for b in range(PACK)]
+        z_banks = [[(cols, product(w2_mx, blocks[0], x_mx, cols, S // 2)) for cols in halves]]
         for t in range(1, PACK):
-            z_banks.append([(slice(0, S), product(w2_mx, planes[t], x_mx, slice(0, S), S))])
+            z_banks.append([(picked, product(w2_mx, blocks[t], x_mx, picked, S))])
 
         w1_grouped = keep.tile([P, PACK * H], BF16, name="w1_grouped", tag="w1_grouped", align_bytes=64)
         for h in range(2):
-            nc.vector.tensor_copy(dealt(w1_grouped)[:, h * 64 : (h + 1) * 64], by_line(w1_raw[h]))
+            nc.vector.tensor_copy(dealt(w1_grouped)[:, h * P // 2 : (h + 1) * P // 2], by_fours(w1_raw[h]))
+        last_z_rows = keep.tile([P, WINDOW], F32, name="last_z_rows", tag="w1_raw1")
+        nc.vector.memset(last_z_rows[:, S:], 0.0)
+        z_rows.append(last_z_rows)
         w1_mx = quantise("w1", w1_grouped[:], H)
-        y_banks = [product(w1_mx, planes[t], x_mx, slice(0, S), S) for t in range(PACK)]
+        y_banks = [product(w1_mx, blocks[t], x_mx, picked, S) for t in range(PACK)]
 
         w3_grouped = keep.tile([P, PACK * N], BF16, name="w3_grouped", align_bytes=64)
         nc.vector.tensor_copy(
-            w3_grouped[:].rearrange("p (c i j) -> p c j i", i=LINE, j=PACK),
-            w3_raw[:].rearrange("p j (c i) -> p c j i", i=LINE),
+            w3_grouped[:].rearrange("p (c i j) -> p c j i", i=RUN, j=PACK),
+            w3_raw[:].rearrange("p j (c i) -> p c j i", i=RUN),
         )
         w3_mx = quantise("w3", w3_grouped[:], N)
-        first_diffs = keep.tile([P, PACK, CHUNKS[0]], F32, name="first_diffs", tag="w1_grouped", align_bytes=64)
 
-        def y_out(t):
-            if Y_OUT[t] == "S":
-                nc.scalar.activation(y_rows[t][:, :S], y_banks[t][:], ACT.Copy, scale=unit_sb[:, t : t + 1])
-            else:
-                nc.vector.tensor_scalar(y_rows[t][:, :S], y_banks[t][:], unit_sb[:, t : t + 1], None, ALU.mult)
+        first_diffs = keep.tile([P, PACK, CHUNKS[0]], F32, name="first_diffs", tag="w1_grouped", align_bytes=64)
 
         r0 = 0
         for c, n in enumerate(CHUNKS):
             last = c == len(CHUNKS) - 1
-            first = s1_sb[:, r0 // 16 : (r0 + n) // 16]
-            second = s2_sb[:, r0 // 16 : (r0 + n) // 16]
+            by_s1 = s1_sb[:, r0 // GROUP : (r0 + n) // GROUP]
+            by_s2 = s2_sb[:, r0 // GROUP : (r0 + n) // GROUP]
+
             diffs = []
             for t in range(PACK):
                 if c == 0:
                     for cols, bank in z_banks[t]:
-                        if Z_OUT[t] == "S":
+                        if t < PACK - 1:
                             nc.scalar.copy(z_rows[t][:, cols], bank[:])
                         else:
                             nc.vector.tensor_copy(z_rows[t][:, cols], bank[:])
-                z2_neg = keep.tile([P, n], F32, name=f"z2_neg{c}_{t}", tag=f"pair{t}")
-                nc.scalar.activation(z2_neg[:], z_rows[t][:].indirect(second), ACT.Copy, scale=-1.0)
+                z2_neg = keep.tile([P, n], F32, name=f"z2_neg{c}_{t}", tag=f"scratch{t}")
+                nc.scalar.activation(z2_neg[:], z_rows[t][:].indirect(by_s2), ACT.Copy, scale=-1.0)
                 if c == 0:
                     diff = first_diffs[:, t, :]
                 else:
                     diff = keep.tile([P, n], F32, name=f"diff{c}_{t}", tag=f"diff{c}_{t}")[:]
-                nc.vector.tensor_tensor(diff, z_rows[t][:].indirect(first), z2_neg[:], ALU.add)
+                nc.vector.tensor_tensor(diff, z_rows[t][:].indirect(by_s1), z2_neg[:], ALU.add)
                 diffs.append(diff)
-                if c == 0 and t >= PACK - Y_EARLY:
-                    y_out(t - (PACK - Y_EARLY))
-            y2_neg = keep.tile([P, PACK, n], F32, name=f"y2_neg{c}")
-            mixed = keep.tile([P, PACK, n], F32, name=f"mixed{c}")
+
+            right = keep.tile([P, PACK, n], F32, name=f"right{c}")
+            left = keep.tile([P, PACK, n], F32, name=f"left{c}")
             for t in range(PACK):
-                if c == 0 and t >= Y_EARLY:
-                    y_out(t)
                 if c == 0:
-                    gate = keep.tile([P, n], F32, name=f"gate{c}_{t}", tag=f"pair{t}")
+                    nc.scalar.activation(y_rows[t][:, :S], y_banks[t][:], ACT.Copy, scale=unit_sb[:, t : t + 1])
+                    gate = keep.tile([P, n], F32, name=f"gate{c}_{t}", tag=f"scratch{t}")
                     nc.scalar.activation(gate[:], diffs[t], ACT.Sigmoid)
                     other_gate = keep.tile([P, n], F32, name=f"other_gate{t}")
                     nc.scalar.activation(other_gate[:], diffs[t], ACT.Sigmoid, scale=-1.0)
-                    nc.vector.tensor_tensor(mixed[:, t, :], y_rows[t][:].indirect(first), gate[:], ALU.mult)
-                    nc.vector.tensor_tensor(y2_neg[:, t, :], y_rows[t][:].indirect(second), other_gate[:], ALU.mult)
+                    nc.vector.tensor_tensor(left[:, t, :], y_rows[t][:].indirect(by_s1), gate[:], ALU.mult)
+                    nc.vector.tensor_tensor(right[:, t, :], y_rows[t][:].indirect(by_s2), other_gate[:], ALU.mult)
                     continue
-                nc.scalar.activation(y2_neg[:, t, :], y_rows[t][:].indirect(second), ACT.Copy, scale=-1.0)
+                nc.scalar.activation(right[:, t, :], y_rows[t][:].indirect(by_s2), ACT.Copy, scale=-1.0)
                 gate = keep.tile([P, n], F32, name=f"gate{c}_{t}")
                 nc.scalar.activation(gate[:], diffs[t], ACT.Sigmoid)
-                y_diff = keep.tile([P, n], F32, name=f"y_diff{c}_{t}", tag=f"pair{t}")
-                if last and t in UNFUSED:
+                y_diff = keep.tile([P, n], F32, name=f"y_diff{c}_{t}", tag=f"scratch{t}")
+                if last:
                     y1 = keep.tile([P, n], F32, name=f"y1_{t}", tag=f"diff{c - 1}_{t}")
-                    nc.scalar.activation(y1[:], y_rows[t][:].indirect(first), ACT.Copy)
-                    nc.vector.tensor_tensor(y_diff[:], y1[:], y2_neg[:, t, :], ALU.add)
+                    nc.scalar.activation(y1[:], y_rows[t][:].indirect(by_s1), ACT.Copy)
+                    nc.vector.tensor_tensor(y_diff[:], y1[:], right[:, t, :], ALU.add)
                 else:
-                    nc.vector.tensor_tensor(y_diff[:], y_rows[t][:].indirect(first), y2_neg[:, t, :], ALU.add)
-                nc.vector.tensor_tensor(mixed[:, t, :], gate[:], y_diff[:], ALU.mult)
+                    nc.vector.tensor_tensor(y_diff[:], y_rows[t][:].indirect(by_s1), right[:, t, :], ALU.add)
+                nc.vector.tensor_tensor(left[:, t, :], gate[:], y_diff[:], ALU.mult)
+
             pieces = [(0, n // 2), (n // 2, n // 2)] if last else [(0, n)]
             hids = []
             for a, w in pieces:
                 hid = keep.tile([P, PACK * w], BF16, name=f"hid{c}_{a}", align_bytes=64)
                 nc.vector.tensor_tensor(
-                    hid[:].rearrange("p (c i t) -> p c t i", i=LINE, t=PACK),
-                    mixed[:, :, a : a + w].rearrange("p t (c i) -> p c t i", i=LINE),
-                    y2_neg[:, :, a : a + w].rearrange("p t (c i) -> p c t i", i=LINE),
+                    hid[:].rearrange("p (c i t) -> p c t i", i=RUN, t=PACK),
+                    left[:, :, a : a + w].rearrange("p t (c i) -> p c t i", i=RUN),
+                    right[:, :, a : a + w].rearrange("p t (c i) -> p c t i", i=RUN),
                     ALU.add if c == 0 else ALU.subtract,
                 )
                 hids.append(hid)
             for (a, w), hid in zip(pieces, hids):
                 hid_mx = quantise(f"hid{c}_{a}", hid[:], w)
                 for m in range(N // P):
-                    bank = product(w3_mx, planes[m], hid_mx, slice(0, w), w)
+                    bank = product(w3_mx, blocks[m], hid_mx, slice(0, w), w)
                     result = keep.tile([P, w], F32, name=f"result{c}_{a}_{m}")
-                    if last and a > 0 and m == 1:
+                    if r0 + a + w == U and m == N // P - 1:
                         nc.vector.tensor_copy(result[:], bank[:])
                     else:
                         nc.scalar.copy(result[:], bank[:])
-                    nc.sync.dma_start(out[planes[m], r0 + a : r0 + a + w], result[:])
+                    nc.sync.dma_start(out[blocks[m], r0 + a : r0 + a + w], result[:])
             r0 = r0 + n

from contextlib import ExitStack

import concourse.mybir as mybir

K, T, S, N, H, U = 512, 2048, 512, 256, 512, 1024
FLOPS = 2 * K * H * S * 2 + 2 * H * N * U

F32 = mybir.dt.float32
BF16 = mybir.dt.bfloat16
I32 = mybir.dt.int32
U32 = mybir.dt.uint32
U16 = mybir.dt.uint16
U8 = mybir.dt.uint8
FP8X4 = mybir.dt.float8_e4m3fn_x4
ALU = mybir.AluOpType
ACT = mybir.ActivationFunctionType

P = 128
PACK = 4
GROUP = 16
QUADRANT = 32
BANKS = 8
WINDOW = S + GROUP
CHUNKS = (256, 512, 256)
RUN = 2


def tile_picked_yfusgat_gate_p_kernel(tc, x_words, x_scales, w1, w2, unit, w3, offs, s1, s2, out):
    nc = tc.nc
    with ExitStack() as ctx:
        keep = ctx.enter_context(tc.tile_pool(name="keep", bufs=1))
        psum = ctx.enter_context(tc.psum_pool(name="psum", bufs=BANKS))

        offs_sb = keep.tile([P, S // GROUP], U16, name="offs_sb")
        s1_sb = keep.tile([P, U // GROUP], U16, name="s1_sb")
        s2_sb = keep.tile([P, U // GROUP], U16, name="s2_sb")
        x_word_table = keep.tile([P, T], I32, name="x_word_table")
        x_scale_table = keep.tile([P, T], U8, name="x_scale_table")
        w1_raw = [keep.tile([P, PACK, H // 2], F32, name=f"w1_raw{h}", tag=f"w1_raw{h}") for h in range(2)]
        w2_raw = [keep.tile([P, PACK, H // 2], F32, name=f"w2_raw{h}") for h in range(2)]
        w3_raw = keep.tile([P, PACK, N], F32, name="w3_raw")
        unit_sb = keep.tile([P, PACK], F32, name="unit_sb")

        nc.gpsimd.memset(x_scale_table[:].bitcast(I32), 0)
        w2_rows = w2.rearrange("(p j) c -> p j c", j=PACK)
        nc.sync.dma_start(w2_raw[0][:], w2_rows[:, :, : H // 2])
        nc.sync.dma_start(offs_sb[:], offs)
        for r in range(PACK):
            nc.sync.dma_start(
                x_scale_table[r:P:QUADRANT, :].bitcast(I32),
                x_scales[0, r : K // 32 : PACK, :].bitcast(I32),
            )
        nc.sync.dma_start(w2_raw[1][:], w2_rows[:, :, H // 2 :])
        nc.sync.dma_start(x_word_table[:], x_words[0].rearrange("p c r -> p (c r)").bitcast(I32))
        w1_rows = w1.rearrange("(p j) c -> p j c", j=PACK)
        nc.sync.dma_start(w1_raw[0][:], w1_rows[:, :, : H // 2])
        nc.sync.dma_start(s2_sb[:], s2)
        nc.sync.dma_start(w1_raw[1][:], w1_rows[:, :, H // 2 :])
        nc.sync.dma_start(s1_sb[:], s1)
        nc.sync.dma_start(unit_sb[:], unit.rearrange("(p t) o -> p (t o)", t=PACK))
        nc.sync.dma_start(w3_raw[:], w3.rearrange("(p j) n -> p j n", j=PACK))

        z_rows = [keep.tile([P, WINDOW], F32, name=f"z_rows{t}") for t in range(PACK - 1)]
        y_rows = [keep.tile([P, WINDOW], F32, name=f"y_rows{t}") for t in range(PACK)]
        for rows in z_rows + y_rows:
            nc.gpsimd.memset(rows[:, S:], 0.0)

        x_scale_picked = keep.tile([P, S], U8, name="x_scale_picked", align_bytes=64)
        x_word_picked = keep.tile([P, S], U32, name="x_word_picked", align_bytes=64)
        nc.vector.tensor_copy(x_scale_picked[:], x_scale_table[:].indirect(offs_sb[:]))

        def quantise(name, grouped, width):
            words = keep.tile([P, width], U32, name=name + "_words", align_bytes=64)
            scales = keep.tile([P, width], U8, name=name + "_scales", align_bytes=64)
            nc.vector.quantize_mx(out=words[:].bitcast(FP8X4), scales=scales[:], in_=grouped)
            return words, scales

        def product(lhs, lhs_cols, rhs, rhs_cols, width):
            bank = psum.tile([P, width], F32, name="bank")
            nc.tensor.matmul_mx(
                out=bank[:],
                lhsT=lhs[0][:, lhs_cols].bitcast(FP8X4),
                lhsT_scale=lhs[1][:, lhs_cols],
                rhs=rhs[0][:, rhs_cols].bitcast(FP8X4),
                rhs_scale=rhs[1][:, rhs_cols],
                start=True,
                stop=True,
            )
            return bank

        def dealt(grouped):
            return grouped[:].rearrange("p (t m j) -> p m j t", t=PACK, j=PACK)

        def by_fours(raw):
            return raw[:].rearrange("p j (m t) -> p m j t", t=PACK)

        w2_grouped = keep.tile([P, PACK * H], BF16, name="w2_grouped", align_bytes=64)
        nc.scalar.copy(dealt(w2_grouped)[:, : P // 2], by_fours(w2_raw[0]))
        nc.vector.tensor_copy(dealt(w2_grouped)[:, P // 2 :], by_fours(w2_raw[1]))
        w2_mx = quantise("w2", w2_grouped[:], H)

        halves = [slice(h * S // 2, (h + 1) * S // 2) for h in range(2)]
        for cols in halves:
            nc.vector.tensor_copy(
                x_word_picked[:, cols],
                x_word_table[:].bitcast(U32).indirect(offs_sb[:, cols.start // GROUP : cols.stop // GROUP]),
            )
        x_mx = (x_word_picked, x_scale_picked)

        picked = slice(0, S)
        blocks = [slice(b * P, (b + 1) * P) for b in range(PACK)]
        z_banks = [[(cols, product(w2_mx, blocks[0], x_mx, cols, S // 2)) for cols in halves]]
        for t in range(1, PACK):
            z_banks.append([(picked, product(w2_mx, blocks[t], x_mx, picked, S))])

        w1_grouped = keep.tile([P, PACK * H], BF16, name="w1_grouped", tag="w1_grouped", align_bytes=64)
        for h in range(2):
            nc.vector.tensor_copy(dealt(w1_grouped)[:, h * P // 2 : (h + 1) * P // 2], by_fours(w1_raw[h]))
        last_z_rows = keep.tile([P, WINDOW], F32, name="last_z_rows", tag="w1_raw1")
        nc.vector.memset(last_z_rows[:, S:], 0.0)
        z_rows.append(last_z_rows)
        w1_mx = quantise("w1", w1_grouped[:], H)
        y_banks = [product(w1_mx, blocks[t], x_mx, picked, S) for t in range(PACK)]

        w3_grouped = keep.tile([P, PACK * N], BF16, name="w3_grouped", align_bytes=64)
        nc.vector.tensor_copy(
            w3_grouped[:].rearrange("p (c i j) -> p c j i", i=RUN, j=PACK),
            w3_raw[:].rearrange("p j (c i) -> p c j i", i=RUN),
        )
        w3_mx = quantise("w3", w3_grouped[:], N)

        first_diffs = keep.tile([P, PACK, CHUNKS[0]], F32, name="first_diffs", tag="w1_grouped", align_bytes=64)

        r0 = 0
        for c, n in enumerate(CHUNKS):
            last = c == len(CHUNKS) - 1
            by_s1 = s1_sb[:, r0 // GROUP : (r0 + n) // GROUP]
            by_s2 = s2_sb[:, r0 // GROUP : (r0 + n) // GROUP]

            diffs = []
            for t in range(PACK):
                if c == 0:
                    for cols, bank in z_banks[t]:
                        if t < PACK - 1:
                            nc.scalar.copy(z_rows[t][:, cols], bank[:])
                        else:
                            nc.vector.tensor_copy(z_rows[t][:, cols], bank[:])
                z2_neg = keep.tile([P, n], F32, name=f"z2_neg{c}_{t}", tag=f"scratch{t}")
                nc.scalar.activation(z2_neg[:], z_rows[t][:].indirect(by_s2), ACT.Copy, scale=-1.0)
                if c == 0:
                    diff = first_diffs[:, t, :]
                else:
                    diff = keep.tile([P, n], F32, name=f"diff{c}_{t}", tag=f"diff{c}_{t}")[:]
                nc.vector.tensor_tensor(diff, z_rows[t][:].indirect(by_s1), z2_neg[:], ALU.add)
                diffs.append(diff)

            right = keep.tile([P, PACK, n], F32, name=f"right{c}")
            left = keep.tile([P, PACK, n], F32, name=f"left{c}")
            for t in range(PACK):
                if c == 0:
                    nc.scalar.activation(y_rows[t][:, :S], y_banks[t][:], ACT.Copy, scale=unit_sb[:, t : t + 1])
                    gate = keep.tile([P, n], F32, name=f"gate{c}_{t}", tag=f"scratch{t}")
                    nc.scalar.activation(gate[:], diffs[t], ACT.Sigmoid)
                    other_gate = keep.tile([P, n], F32, name=f"other_gate{t}")
                    nc.scalar.activation(other_gate[:], diffs[t], ACT.Sigmoid, scale=-1.0)
                    nc.vector.tensor_tensor(left[:, t, :], y_rows[t][:].indirect(by_s1), gate[:], ALU.mult)
                    nc.vector.tensor_tensor(right[:, t, :], y_rows[t][:].indirect(by_s2), other_gate[:], ALU.mult)
                    continue
                nc.scalar.activation(right[:, t, :], y_rows[t][:].indirect(by_s2), ACT.Copy, scale=-1.0)
                gate = keep.tile([P, n], F32, name=f"gate{c}_{t}")
                nc.scalar.activation(gate[:], diffs[t], ACT.Sigmoid)
                y_diff = keep.tile([P, n], F32, name=f"y_diff{c}_{t}", tag=f"scratch{t}")
                if last:
                    y1 = keep.tile([P, n], F32, name=f"y1_{t}", tag=f"diff{c - 1}_{t}")
                    nc.scalar.activation(y1[:], y_rows[t][:].indirect(by_s1), ACT.Copy)
                    nc.vector.tensor_tensor(y_diff[:], y1[:], right[:, t, :], ALU.add)
                else:
                    nc.vector.tensor_tensor(y_diff[:], y_rows[t][:].indirect(by_s1), right[:, t, :], ALU.add)
                nc.vector.tensor_tensor(left[:, t, :], gate[:], y_diff[:], ALU.mult)

            pieces = [(0, n // 2), (n // 2, n // 2)] if last else [(0, n)]
            hids = []
            for a, w in pieces:
                hid = keep.tile([P, PACK * w], BF16, name=f"hid{c}_{a}", align_bytes=64)
                nc.vector.tensor_tensor(
                    hid[:].rearrange("p (c i t) -> p c t i", i=RUN, t=PACK),
                    left[:, :, a : a + w].rearrange("p t (c i) -> p c t i", i=RUN),
                    right[:, :, a : a + w].rearrange("p t (c i) -> p c t i", i=RUN),
                    ALU.add if c == 0 else ALU.subtract,
                )
                hids.append(hid)
            for (a, w), hid in zip(pieces, hids):
                hid_mx = quantise(f"hid{c}_{a}", hid[:], w)
                for m in range(N // P):
                    bank = product(w3_mx, blocks[m], hid_mx, slice(0, w), w)
                    result = keep.tile([P, w], F32, name=f"result{c}_{a}_{m}")
                    if r0 + a + w == U and m == N // P - 1:
                        nc.vector.tensor_copy(result[:], bank[:])
                    else:
                        nc.scalar.copy(result[:], bank[:])
                    nc.sync.dma_start(out[blocks[m], r0 + a : r0 + a + w], result[:])
            r0 = r0 + n
